import numpy as np
import ml_dtypes


def mxq(x, axis, fmt="e4m3"):
    dtype, down = {"e4m3": (ml_dtypes.float8_e4m3fn, 7), "e5m2": (ml_dtypes.float8_e5m2, 14)}[fmt]
    v = np.moveaxis(np.asarray(x, np.float32).astype(ml_dtypes.bfloat16).astype(np.float64), axis, -1)
    blocks = v.reshape(v.shape[:-1] + (-1, 32))
    amax = np.abs(blocks).max(-1, keepdims=True)
    byte = np.maximum(np.where(amax > 0, np.frexp(amax)[1] - 1 + 127, 0) - down, 1)
    scale = np.exp2(byte - 127.0)
    codes = (blocks / scale).astype(np.float32).astype(dtype).astype(np.float64)
    return np.moveaxis((codes * scale).reshape(v.shape), -1, axis)


WIDE = False


def mx_kscale(k):
    if not WIDE:
        return np.ones(k)
    levels = np.array([10, -10, 5, -5, 0])
    if k % 512:
        return np.exp2(np.random.permutation(np.resize(levels, k // 32))).repeat(32)
    a = np.empty((k // 512, 16))
    for p in range(k // 512):
        a[p, :8] = np.random.permutation(np.resize(levels, 8))
        for g in range(8):
            far = levels[np.abs(levels - a[p, g]) >= 10]
            a[p, g + 8] = far[np.random.randint(len(far))]
    return np.exp2(a.ravel()).repeat(32)


def f64(x):
    return np.asarray(x).astype(np.float64)


def striped(idx):
    return np.tile(idx.reshape(-1, 16).T, (8, 1)).astype(np.uint16)


def unstriped(offs):
    return offs[:16].T.reshape(-1).astype(np.int64)


def striped8(idx):
    return np.concatenate([x.reshape(-1, 16).T for x in idx]).astype(np.uint16)


def runs(offs, k):
    lists = np.stack([offs[16 * r : 16 * r + 16].T.reshape(-1) for r in range(8)]).astype(np.int64)
    return lists[np.arange(k) % 512 // 64]


def pack_weight(w):
    k, n = w.shape
    w = f64(np.asarray(w, np.float32).astype(ml_dtypes.bfloat16)).reshape(k // 32, 32, n)
    amax = np.abs(w).max(1)
    byte = np.clip(np.where(amax > 0, np.frexp(amax)[1] - 1 + 127 - 7, 1), 1, 254)
    scaled = (w * np.exp2(127.0 - byte)[:, None, :]).reshape(k, n).astype(np.float32)
    words = np.ascontiguousarray(scaled.reshape(k // 512, 128, 4, n).transpose(0, 1, 3, 2)).astype(ml_dtypes.float8_e4m3fn).view(np.uint8)
    return words, np.ascontiguousarray(byte.astype(np.uint8).reshape(k // 512, 16, n))


def unpack_weight(words, scales):
    g, p, n, _ = words.shape
    vals = np.ascontiguousarray(words).view(ml_dtypes.float8_e4m3fn).astype(np.float64) * np.repeat(np.exp2(scales.astype(np.float64) - 127.0), 8, axis=1)[..., None]
    return vals.transpose(0, 1, 3, 2).reshape(g * 512, n)


def relu(v):
    return np.maximum(v, 0.0)

def planes(y):
    n, m = y.shape
    v = y.astype(np.float32).astype(ml_dtypes.bfloat16).astype(np.float64).reshape(n // 32, 32, m)
    top = np.abs(v).max(1)
    byte = np.clip(np.where(top > 0, np.frexp(top)[1] - 1 + 127 - 7, 1), 1, 254)
    codes = (v * np.exp2(127.0 - byte)[:, None, :]).reshape(n, m).astype(np.float32).astype(ml_dtypes.float8_e4m3fn).view(np.uint8)
    words = codes.reshape(n // 512, 128, 4, m).transpose(0, 1, 3, 2)
    return np.ascontiguousarray(words), np.ascontiguousarray(byte.astype(np.uint8).reshape(n // 512, 16, m))


K, T, S, H, G = 512, 2048, 512, 512, 2048


def setup_inputs():
    n = np.random.standard_normal
    s = mx_kscale(K)[:, None]
    packed_xT = pack_weight(n((K, T)) * s)
    packed_w1 = pack_weight(n((K, H)) / np.sqrt(K) / s)
    packed_dT = pack_weight(n((K, G)) / s)
    return {
        "x_words": packed_xT[0],
        "x_scales": packed_xT[1],
        "w1_words": packed_w1[0],
        "w1_scales": packed_w1[1],
        "gs": (np.random.uniform(0.5, 1.5, (K, 1)) * s).astype(np.float32),
        "d_words": packed_dT[0],
        "d_scales": packed_dT[1],
        "offs": striped(np.random.permutation(T)[:S]),
        "n1": striped8(np.stack([np.random.permutation(S) for _ in range(8)])),
        "k1": striped8(np.random.randint(0, G, (8, H))),
        "n2": striped8(np.stack([np.random.permutation(S) for _ in range(8)])),
        "n3": striped8(np.stack([np.random.permutation(S) for _ in range(8)])),
    }


def reference(x_words, x_scales, w1_words, w1_scales, gs, d_words, d_scales, offs, n1, k1, n2, n3):
    d_k1 = unpack_weight(d_words, d_scales)[np.arange(K)[:, None], runs(k1, K)]
    xq = unpack_weight(x_words, x_scales)[:, unstriped(offs)]
    y = unpack_weight(w1_words, w1_scales).T @ xq
    rl = relu(y)
    ds = np.zeros((H, S))
    ds[np.arange(H)[:, None], runs(n1, H)] = rl
    z = f64(gs) * (ds - (0.5 * y))
    h = 0.0625 * ((d_k1.T @ mxq(z, 0, "e4m3")))
    out_0 = h * (h[np.arange(H)[:, None], runs(n2, H)] - (h[np.arange(H)[:, None], runs(n3, H)]))
    return (out_0,) + planes(out_0)

@@ -1,0 +1,216 @@
+from contextlib import ExitStack
+
+import concourse.mybir as mybir
+
+K, T, S, H, G = 512, 2048, 512, 512, 2048
+FLOPS = 2 * K * H * S + 2 * H * H * S
+
+F32 = mybir.dt.float32
+BF16 = mybir.dt.bfloat16
+I32 = mybir.dt.int32
+U32 = mybir.dt.uint32
+U16 = mybir.dt.uint16
+U8 = mybir.dt.uint8
+FP8X4 = mybir.dt.float8_e4m3fn_x4
+ALU = mybir.AluOpType
+ACT = mybir.ActivationFunctionType
+
+P = 128
+PACK = 4
+HALF = S // 2
+LIST = 16
+OUT_CHUNKS = ((0, 256), (256, 128), (384, 128))
+
+
+def tile_picked_densesendwind_none_po_kernel(
+    tc, x_words, x_scales, w1_words, w1_scales, gs, d_words, d_scales, offs, n1, k1, n2, n3, out_0, out_1, out_2
+):
+    nc = tc.nc
+
+    def words_of(dram):
+        return dram[0].rearrange("p c r -> p (c r)").bitcast(I32)
+
+    def entries(lists, first, count):
+        return lists[:, first // LIST : (first + count) // LIST]
+
+    with ExitStack() as ctx:
+        keep = ctx.enter_context(tc.tile_pool(name="keep", bufs=1))
+        psum = ctx.enter_context(tc.psum_pool(name="psum", bufs=8))
+
+        offs_sb = keep.tile([P, S // LIST], U16)
+        n1_sb = keep.tile([P, S // LIST], U16)
+        k1_sb = keep.tile([P, H // LIST], U16)
+        n2_sb = keep.tile([P, S // LIST], U16)
+        n3_sb = keep.tile([P, S // LIST], U16)
+
+        x_table = keep.tile([P, T], U32, align_bytes=64)
+        xs_table = keep.tile([P, T], U8, align_bytes=64)
+        w1_raw = keep.tile([P, H], U32, align_bytes=64)
+        w1s_raw = keep.tile([P, H], U8, align_bytes=64)
+        d_table = keep.tile([P, G], U32, align_bytes=64)
+        dsc_table = keep.tile([P, G], U8, align_bytes=64)
+        d_plane = keep.tile([P, H], U8, align_bytes=64)
+        gs_sb = keep.tile([P, PACK], F32)
+
+        nc.vector.memset(d_plane[:].bitcast(I32), 0)
+
+        def load_plane(dst, scales, q):
+            rows = scales[0, 4 * q : 4 * q + 4, :].bitcast(I32)
+            nc.sync.dma_start(
+                out=dst[32 * q : 32 * q + 32, :].bitcast(I32),
+                in_=rows.unsqueeze(0).broadcast_to([8, 4, rows.shape[1]]),
+            )
+
+        for q in range(4):
+            load_plane(xs_table, x_scales, q)
+        nc.sync.dma_start(offs_sb[:], offs)
+        nc.sync.dma_start(out=w1_raw[:].bitcast(I32), in_=words_of(w1_words))
+        nc.sync.dma_start(out=x_table[:].bitcast(I32), in_=words_of(x_words))
+        for q in range(4):
+            load_plane(w1s_raw, w1_scales, q)
+        nc.sync.dma_start(out=gs_sb[:], in_=gs.rearrange("(p t) o -> p (t o)", t=PACK))
+        nc.sync.dma_start(n1_sb[:], n1)
+        nc.sync.dma_start(k1_sb[:], k1)
+        nc.sync.dma_start(
+            out=dsc_table[:].bitcast(I32), in_=d_scales[0].bitcast(I32).unsqueeze(1).broadcast_to([16, 8, G // 4])
+        )
+        nc.sync.dma_start(out=d_table[:].bitcast(I32), in_=words_of(d_words))
+        nc.sync.dma_start(n3_sb[:], n3)
+        nc.sync.dma_start(n2_sb[:], n2)
+
+        half_gs = keep.tile([P, PACK], F32)
+        nc.scalar.activation(half_gs[:], gs_sb[:], ACT.Copy, scale=-0.5)
+
+        def deal(dst, src):
+            nc.vector.tensor_copy(
+                out=dst[:].rearrange("p (t m) -> p t m", t=PACK), in_=src[:].rearrange("p (m t) -> p t m", t=PACK)
+            )
+
+        xs = keep.tile([P, S], U8, align_bytes=64)
+        nc.vector.tensor_copy(xs[:], xs_table[:].indirect(offs_sb[:]))
+        w1 = keep.tile([P, H], U32, align_bytes=64)
+        w1s = keep.tile([P, H], U8, align_bytes=64)
+        deal(w1, w1_raw)
+        deal(w1s, w1s_raw)
+        xq = keep.tile([P, S], U32, align_bytes=64)
+        for c in (0, HALF):
+            nc.vector.tensor_copy(xq[:, c : c + HALF], x_table[:].indirect(entries(offs_sb, c, HALF)))
+
+        def product(lhs, lhs_scales, t, rhs, rhs_scales, first, count):
+            acc = psum.tile([P, S], F32, name="acc")
+            rows = slice(P * t, P * (t + 1))
+            cols = slice(first, first + count)
+            nc.tensor.matmul_mx(
+                out=acc[:, 0:count],
+                lhsT=lhs[:, rows].bitcast(FP8X4),
+                lhsT_scale=lhs_scales[:, rows],
+                rhs=rhs[:, cols].bitcast(FP8X4),
+                rhs_scale=rhs_scales[:, cols],
+                start=True,
+                stop=True,
+            )
+            return acc[:, 0:count]
+
+        rl = keep.tile([P, PACK, S], F32)
+        yh = keep.tile([P, PACK, S], F32)
+        sent = [keep.tile([P, 2 * S], F32, name=f"sent{t}") for t in range(PACK)]
+        z_rows = keep.tile([P, PACK, S], BF16, align_bytes=64)
+
+        def send(t, first, count):
+            cols = slice(first, first + count)
+            y = product(w1, w1s, t, xq, xs, first, count)
+            nc.scalar.activation(rl[:, t, cols], y, ACT.Relu)
+            nc.vector.tensor_copy(sent[t][:].indirect(entries(n1_sb, first, count)), rl[:, t, cols])
+            nc.scalar.activation(yh[:, t, cols], y, ACT.Copy, scale=half_gs[:, t : t + 1])
+
+        def combine(t, first, count):
+            cols = slice(first, first + count)
+            nc.vector.scalar_tensor_tensor(
+                z_rows[:, t, cols], sent[t][:, cols], gs_sb[:, t : t + 1], yh[:, t, cols], ALU.mult, ALU.add
+            )
+
+        for c in (0, HALF):
+            send(0, c, HALF)
+            send(1, c, HALF)
+
+        ds_picked = keep.tile([P, H], U8, align_bytes=64)
+        nc.vector.tensor_copy(ds_picked[:], dsc_table[:].indirect(k1_sb[:]))
+        combine(0, 0, S)
+        ds_dealt = keep.tile([P, H], U8, align_bytes=64)
+        deal(ds_dealt, ds_picked)
+        for r in range(4):
+            nc.sync.dma_start(out=d_plane[r:P:32, :].bitcast(I32), in_=ds_dealt[8 * r : P : 32, :].bitcast(I32))
+        send(2, 0, S)
+        d_picked = keep.tile([P, H], U32, align_bytes=64)
+        nc.vector.tensor_copy(d_picked[:], d_table[:].indirect(k1_sb[:]))
+        combine(1, 0, S)
+        dq = keep.tile([P, H], U32, align_bytes=64)
+        deal(dq, d_picked)
+        combine(2, 0, S)
+        send(3, 0, S)
+
+        z_woven = [keep.tile([P, HALF, PACK], BF16, name=f"z_woven{i}", align_bytes=64) for i in range(2)]
+        zq = keep.tile([P, S], U32, align_bytes=64)
+        zs = keep.tile([P, S], U8, align_bytes=64)
+        combine(3, 0, HALF)
+        nc.scalar.copy(z_woven[0][:], z_rows[:, :, 0:HALF].rearrange("p t j -> p j t"))
+        combine(3, HALF, HALF)
+        nc.vector.tensor_copy(z_woven[1][:], z_rows[:, :, HALF:S].rearrange("p t j -> p j t"))
+
+        h = [keep.tile([P, S], F32, name=f"h{t}") for t in range(PACK)]
+        h_all = keep.tile([P, PACK, S], F32)
+        later = []
+        for i in (1, 0):
+            cols = slice(i * HALF, (i + 1) * HALF)
+            nc.vector.quantize_mx(
+                out=zq[:, cols].bitcast(FP8X4), scales=zs[:, cols], in_=z_woven[i][:].rearrange("p j t -> p (j t)")
+            )
+            acc = product(dq, d_plane, 0, zq, zs, i * HALF, HALF)
+            nc.scalar.activation(h[0][:, cols], acc, ACT.Copy, scale=0.0625)
+            later.append((h_all[:, 0, cols], acc))
+        for t in range(1, PACK):
+            acc = product(dq, d_plane, t, zq, zs, 0, S)
+            nc.scalar.activation(h[t][:], acc, ACT.Copy, scale=0.0625)
+            later.append((h_all[:, t, :], acc))
+        for dst, acc in later:
+            nc.scalar.activation(dst, acc, ACT.Copy, scale=0.0625)
+
+        out_rows = out_0.rearrange("(p t) j -> p t j", t=PACK)
+        out_words = words_of(out_1)
+        oq = keep.tile([P, S], U32, align_bytes=64)
+        os_plane = keep.tile([P, S], U8, align_bytes=64)
+
+        def hand_on(woven, cols):
+            nc.vector.quantize_mx(
+                out=oq[:, cols].bitcast(FP8X4), scales=os_plane[:, cols], in_=woven[:].rearrange("p j t -> p (j t)")
+            )
+            nc.scalar.dma_start(out=out_words[:, cols], in_=oq[:, cols].bitcast(I32))
+
+        waiting = None
+        for first, count in OUT_CHUNKS:
+            cols = slice(first, first + count)
+            at3 = keep.tile([P, PACK, count], F32, name=f"at3_{first}")
+            diff = keep.tile([P, PACK, count], F32, name=f"diff_{first}")
+            res = keep.tile([P, PACK, count], F32, name=f"res_{first}")
+            woven = keep.tile([P, count, PACK], BF16, name=f"woven_{first}", align_bytes=64)
+            for t in range(PACK):
+                nc.vector.tensor_copy(at3[:, t, :], h[t][:].indirect(entries(n3_sb, first, count)))
+            for t in range(PACK):
+                nc.vector.tensor_tensor(
+                    diff[:, t, :], h[t][:].indirect(entries(n2_sb, first, count)), at3[:, t, :], ALU.subtract
+                )
+            if waiting is not None:
+                hand_on(*waiting)
+            nc.vector.tensor_tensor(res[:], diff[:], h_all[:, :, cols], ALU.mult)
+            nc.sync.dma_start(out=out_rows[:, :, cols], in_=res[:])
+            if first + count < S:
+                nc.scalar.copy(woven[:], res[:].rearrange("p t j -> p j t"))
+            else:
+                nc.vector.tensor_copy(woven[:], res[:].rearrange("p t j -> p j t"))
+            waiting = (woven, cols)
+        hand_on(*waiting)
+        for q in range(4):
+            queue = nc.sync if q % 2 == 0 else nc.scalar
+            queue.dma_start(
+                out=out_2[0, 4 * q : 4 * q + 4, :].bitcast(I32), in_=os_plane[32 * q : 32 * q + 4, :].bitcast(I32)
+            )

@@ -18,8 +18,9 @@ ACT = mybir.ActivationFunctionType
 P = 128
 PACK = 4
 HALF = S // 2
+LAST = PACK - 1
 LIST = 16
-OUT_CHUNKS = ((0, 256), (256, 128), (384, 128))
+OUT_CHUNKS = ((0, 160), (160, 160), (320, 192))
 
 
 def tile_picked_densesendwind_none_po_kernel(
@@ -52,6 +53,7 @@ def tile_picked_densesendwind_none_po_kernel(
         d_plane = keep.tile([P, H], U8, align_bytes=64)
         gs_sb = keep.tile([P, PACK], F32)
 
+        nc.vector.memset(dsc_table[:].bitcast(I32), 0)
         nc.vector.memset(d_plane[:].bitcast(I32), 0)
 
         def load_plane(dst, scales, q):
@@ -64,16 +66,14 @@ def tile_picked_densesendwind_none_po_kernel(
         for q in range(4):
             load_plane(xs_table, x_scales, q)
         nc.sync.dma_start(offs_sb[:], offs)
-        nc.sync.dma_start(out=w1_raw[:].bitcast(I32), in_=words_of(w1_words))
+        nc.sync.dma_start(k1_sb[:], k1)
+        nc.sync.dma_start(out=dsc_table[0:P:8, :].bitcast(I32), in_=d_scales[0].bitcast(I32))
         nc.sync.dma_start(out=x_table[:].bitcast(I32), in_=words_of(x_words))
+        nc.sync.dma_start(out=w1_raw[:].bitcast(I32), in_=words_of(w1_words))
         for q in range(4):
             load_plane(w1s_raw, w1_scales, q)
-        nc.sync.dma_start(out=gs_sb[:], in_=gs.rearrange("(p t) o -> p (t o)", t=PACK))
         nc.sync.dma_start(n1_sb[:], n1)
-        nc.sync.dma_start(k1_sb[:], k1)
-        nc.sync.dma_start(
-            out=dsc_table[:].bitcast(I32), in_=d_scales[0].bitcast(I32).unsqueeze(1).broadcast_to([16, 8, G // 4])
-        )
+        nc.sync.dma_start(out=gs_sb[:], in_=gs.rearrange("(p t) o -> p (t o)", t=PACK))
         nc.sync.dma_start(out=d_table[:].bitcast(I32), in_=words_of(d_words))
         nc.sync.dma_start(n3_sb[:], n3)
         nc.sync.dma_start(n2_sb[:], n2)
@@ -81,20 +81,29 @@ def tile_picked_densesendwind_none_po_kernel(
         half_gs = keep.tile([P, PACK], F32)
         nc.scalar.activation(half_gs[:], gs_sb[:], ACT.Copy, scale=-0.5)
 
-        def deal(dst, src):
+        def deal(dst, src, first, last):
             nc.vector.tensor_copy(
-                out=dst[:].rearrange("p (t m) -> p t m", t=PACK), in_=src[:].rearrange("p (m t) -> p t m", t=PACK)
+                out=dst[:].rearrange("p (t m) -> p t m", t=PACK)[:, first:last, :],
+                in_=src[:].rearrange("p (m t) -> p t m", t=PACK)[:, first:last, :],
             )
 
         xs = keep.tile([P, S], U8, align_bytes=64)
         nc.vector.tensor_copy(xs[:], xs_table[:].indirect(offs_sb[:]))
         w1 = keep.tile([P, H], U32, align_bytes=64)
         w1s = keep.tile([P, H], U8, align_bytes=64)
-        deal(w1, w1_raw)
-        deal(w1s, w1s_raw)
+        ds_picked = keep.tile([P, H], U8, align_bytes=64)
+        nc.vector.tensor_copy(ds_picked[:], dsc_table[:].indirect(k1_sb[:]))
         xq = keep.tile([P, S], U32, align_bytes=64)
-        for c in (0, HALF):
-            nc.vector.tensor_copy(xq[:, c : c + HALF], x_table[:].indirect(entries(offs_sb, c, HALF)))
+        nc.vector.tensor_copy(xq[:, 0:HALF], x_table[:].indirect(entries(offs_sb, 0, HALF)))
+        deal(w1, w1_raw, 0, 2)
+        deal(w1s, w1s_raw, 0, 2)
+        nc.vector.tensor_copy(xq[:, HALF:S], x_table[:].indirect(entries(offs_sb, HALF, HALF)))
+        deal(w1, w1_raw, 2, PACK)
+        deal(w1s, w1s_raw, 2, PACK)
+        ds_dealt = keep.tile([P, H], U8, align_bytes=64)
+        deal(ds_dealt, ds_picked, 0, PACK)
+        for r in range(4):
+            nc.sync.dma_start(out=d_plane[r:P:32, :].bitcast(I32), in_=ds_dealt[8 * r : P : 32, :].bitcast(I32))
 
         def product(lhs, lhs_scales, t, rhs, rhs_scales, first, count):
             acc = psum.tile([P, S], F32, name="acc")
@@ -121,7 +130,8 @@ def tile_picked_densesendwind_none_po_kernel(
             y = product(w1, w1s, t, xq, xs, first, count)
             nc.scalar.activation(rl[:, t, cols], y, ACT.Relu)
             nc.vector.tensor_copy(sent[t][:].indirect(entries(n1_sb, first, count)), rl[:, t, cols])
-            nc.scalar.activation(yh[:, t, cols], y, ACT.Copy, scale=half_gs[:, t : t + 1])
+            half = half_gs[:, t : t + 1] if t == LAST else -0.5
+            nc.scalar.activation(yh[:, t, cols], y, ACT.Copy, scale=half)
 
         def combine(t, first, count):
             cols = slice(first, first + count)
@@ -129,32 +139,32 @@ def tile_picked_densesendwind_none_po_kernel(
                 z_rows[:, t, cols], sent[t][:, cols], gs_sb[:, t : t + 1], yh[:, t, cols], ALU.mult, ALU.add
             )
 
+        unscaled = keep.tile([P, LAST, S], F32)
+
+        def combine_aside(t):
+            nc.gpsimd.tensor_tensor(unscaled[:, t, :], sent[t][:, 0:S], yh[:, t, :], ALU.add)
+            nc.scalar.activation(z_rows[:, t, :], unscaled[:, t, :], ACT.Copy, scale=gs_sb[:, t : t + 1])
+
         for c in (0, HALF):
             send(0, c, HALF)
             send(1, c, HALF)
-
-        ds_picked = keep.tile([P, H], U8, align_bytes=64)
-        nc.vector.tensor_copy(ds_picked[:], dsc_table[:].indirect(k1_sb[:]))
-        combine(0, 0, S)
-        ds_dealt = keep.tile([P, H], U8, align_bytes=64)
-        deal(ds_dealt, ds_picked)
-        for r in range(4):
-            nc.sync.dma_start(out=d_plane[r:P:32, :].bitcast(I32), in_=ds_dealt[8 * r : P : 32, :].bitcast(I32))
         send(2, 0, S)
+        combine_aside(0)
+        combine_aside(1)
         d_picked = keep.tile([P, H], U32, align_bytes=64)
         nc.vector.tensor_copy(d_picked[:], d_table[:].indirect(k1_sb[:]))
-        combine(1, 0, S)
-        dq = keep.tile([P, H], U32, align_bytes=64)
-        deal(dq, d_picked)
-        combine(2, 0, S)
         send(3, 0, S)
+        combine_aside(2)
+        dq = keep.tile([P, H], U32, align_bytes=64)
+        deal(dq, d_picked, 0, PACK)
 
         z_woven = [keep.tile([P, HALF, PACK], BF16, name=f"z_woven{i}", align_bytes=64) for i in range(2)]
         zq = keep.tile([P, S], U32, align_bytes=64)
         zs = keep.tile([P, S], U8, align_bytes=64)
-        combine(3, 0, HALF)
-        nc.scalar.copy(z_woven[0][:], z_rows[:, :, 0:HALF].rearrange("p t j -> p j t"))
-        combine(3, HALF, HALF)
+        nc.scalar.copy(z_woven[0][:, :, 0:LAST], z_rows[:, 0:LAST, 0:HALF].rearrange("p t j -> p j t"))
+        combine(LAST, HALF, HALF)
+        combine(LAST, 0, HALF)
+        nc.scalar.copy(z_woven[0][:, :, LAST], z_rows[:, LAST, 0:HALF])
         nc.vector.tensor_copy(z_woven[1][:], z_rows[:, :, HALF:S].rearrange("p t j -> p j t"))
 
         h = [keep.tile([P, S], F32, name=f"h{t}") for t in range(PACK)]
@@ -180,35 +190,46 @@ def tile_picked_densesendwind_none_po_kernel(
         oq = keep.tile([P, S], U32, align_bytes=64)
         os_plane = keep.tile([P, S], U8, align_bytes=64)
 
-        def hand_on(woven, cols):
+        woven = [keep.tile([P, HALF, PACK], BF16, name=f"woven{i}", align_bytes=64) for i in range(2)]
+
+        def weave(engine_copy, res, first, count):
+            for i in range(2):
+                lo, hi = max(first, i * HALF), min(first + count, (i + 1) * HALF)
+                if lo < hi:
+                    engine_copy(
+                        woven[i][:, lo - i * HALF : hi - i * HALF, :],
+                        res[:, :, lo - first : hi - first].rearrange("p t j -> p j t"),
+                    )
+
+        def hand_on(i):
+            cols = slice(i * HALF, (i + 1) * HALF)
             nc.vector.quantize_mx(
-                out=oq[:, cols].bitcast(FP8X4), scales=os_plane[:, cols], in_=woven[:].rearrange("p j t -> p (j t)")
+                out=oq[:, cols].bitcast(FP8X4), scales=os_plane[:, cols], in_=woven[i][:].rearrange("p j t -> p (j t)")
             )
             nc.scalar.dma_start(out=out_words[:, cols], in_=oq[:, cols].bitcast(I32))
 
-        waiting = None
         for first, count in OUT_CHUNKS:
             cols = slice(first, first + count)
             at3 = keep.tile([P, PACK, count], F32, name=f"at3_{first}")
             diff = keep.tile([P, PACK, count], F32, name=f"diff_{first}")
             res = keep.tile([P, PACK, count], F32, name=f"res_{first}")
-            woven = keep.tile([P, count, PACK], BF16, name=f"woven_{first}", align_bytes=64)
+            last = first + count == S
             for t in range(PACK):
                 nc.vector.tensor_copy(at3[:, t, :], h[t][:].indirect(entries(n3_sb, first, count)))
             for t in range(PACK):
                 nc.vector.tensor_tensor(
                     diff[:, t, :], h[t][:].indirect(entries(n2_sb, first, count)), at3[:, t, :], ALU.subtract
                 )
-            if waiting is not None:
-                hand_on(*waiting)
-            nc.vector.tensor_tensor(res[:], diff[:], h_all[:, :, cols], ALU.mult)
-            nc.sync.dma_start(out=out_rows[:, :, cols], in_=res[:])
-            if first + count < S:
-                nc.scalar.copy(woven[:], res[:].rearrange("p t j -> p j t"))
+            if last:
+                for pair in (slice(0, 2), slice(2, 4)):
+                    nc.vector.tensor_tensor(res[:, pair, :], diff[:, pair, :], h_all[:, pair, cols], ALU.mult)
+                    nc.sync.dma_start(out=out_rows[:, pair, cols], in_=res[:, pair, :])
+                hand_on(0)
             else:
-                nc.vector.tensor_copy(woven[:], res[:].rearrange("p t j -> p j t"))
-            waiting = (woven, cols)
-        hand_on(*waiting)
+                nc.gpsimd.tensor_tensor(res[:], diff[:], h_all[:, :, cols], ALU.mult)
+                nc.sync.dma_start(out=out_rows[:, :, cols], in_=res[:])
+            weave(nc.vector.tensor_copy if last else nc.scalar.copy, res, first, count)
+        hand_on(1)
         for q in range(4):
             queue = nc.sync if q % 2 == 0 else nc.scalar
             queue.dma_start(

@@ -20,7 +20,6 @@ PACK = 4
 HALF = S // 2
 LAST = PACK - 1
 LIST = 16
-OUT_CHUNKS = ((0, 160), (160, 160), (320, 192))
 
 
 def tile_picked_densesendwind_none_po_kernel(
@@ -63,11 +62,11 @@ def tile_picked_densesendwind_none_po_kernel(
                 in_=rows.unsqueeze(0).broadcast_to([8, 4, rows.shape[1]]),
             )
 
+        nc.sync.dma_start(k1_sb[:], k1)
+        nc.sync.dma_start(out=dsc_table[0:P:8, :].bitcast(I32), in_=d_scales[0].bitcast(I32))
         for q in range(4):
             load_plane(xs_table, x_scales, q)
         nc.sync.dma_start(offs_sb[:], offs)
-        nc.sync.dma_start(k1_sb[:], k1)
-        nc.sync.dma_start(out=dsc_table[0:P:8, :].bitcast(I32), in_=d_scales[0].bitcast(I32))
         nc.sync.dma_start(out=x_table[:].bitcast(I32), in_=words_of(x_words))
         nc.sync.dma_start(out=w1_raw[:].bitcast(I32), in_=words_of(w1_words))
         for q in range(4):
@@ -83,36 +82,41 @@ def tile_picked_densesendwind_none_po_kernel(
 
         def deal(dst, src, first, last):
             nc.vector.tensor_copy(
-                out=dst[:].rearrange("p (t m) -> p t m", t=PACK)[:, first:last, :],
+                out=dst.rearrange("p (t c i) -> p c t i", t=last - first, i=PACK),
+                in_=src[:].rearrange("p (c i t) -> p c t i", t=PACK, i=PACK)[:, :, first:last, :],
+            )
+
+        def deal_bytes(dst, src, first, last):
+            nc.vector.tensor_copy(
+                out=dst.rearrange("p (t m) -> p t m", t=last - first),
                 in_=src[:].rearrange("p (m t) -> p t m", t=PACK)[:, first:last, :],
             )
 
+        ds_picked = keep.tile([P, H], U8, align_bytes=64)
+        nc.vector.tensor_copy(ds_picked[:], dsc_table[:].indirect(k1_sb[:]))
         xs = keep.tile([P, S], U8, align_bytes=64)
         nc.vector.tensor_copy(xs[:], xs_table[:].indirect(offs_sb[:]))
         w1 = keep.tile([P, H], U32, align_bytes=64)
         w1s = keep.tile([P, H], U8, align_bytes=64)
-        ds_picked = keep.tile([P, H], U8, align_bytes=64)
-        nc.vector.tensor_copy(ds_picked[:], dsc_table[:].indirect(k1_sb[:]))
+        ds_dealt = keep.tile([P, H], U8, align_bytes=64)
+        deal_bytes(ds_dealt[:], ds_picked, 0, PACK)
         xq = keep.tile([P, S], U32, align_bytes=64)
         nc.vector.tensor_copy(xq[:, 0:HALF], x_table[:].indirect(entries(offs_sb, 0, HALF)))
-        deal(w1, w1_raw, 0, 2)
-        deal(w1s, w1s_raw, 0, 2)
+        deal(w1[:, 0 : 2 * P], w1_raw, 0, 2)
+        deal_bytes(w1s[:, 0 : 2 * P], w1s_raw, 0, 2)
         nc.vector.tensor_copy(xq[:, HALF:S], x_table[:].indirect(entries(offs_sb, HALF, HALF)))
-        deal(w1, w1_raw, 2, PACK)
-        deal(w1s, w1s_raw, 2, PACK)
-        ds_dealt = keep.tile([P, H], U8, align_bytes=64)
-        deal(ds_dealt, ds_picked, 0, PACK)
+        deal(w1[:, 2 * P : H], w1_raw, 2, PACK)
+        deal_bytes(w1s[:, 2 * P : H], w1s_raw, 2, PACK)
         for r in range(4):
             nc.sync.dma_start(out=d_plane[r:P:32, :].bitcast(I32), in_=ds_dealt[8 * r : P : 32, :].bitcast(I32))
 
-        def product(lhs, lhs_scales, t, rhs, rhs_scales, first, count):
+        def product(lhs, lhs_scales, rhs, rhs_scales, first, count):
             acc = psum.tile([P, S], F32, name="acc")
-            rows = slice(P * t, P * (t + 1))
             cols = slice(first, first + count)
             nc.tensor.matmul_mx(
                 out=acc[:, 0:count],
-                lhsT=lhs[:, rows].bitcast(FP8X4),
-                lhsT_scale=lhs_scales[:, rows],
+                lhsT=lhs.bitcast(FP8X4),
+                lhsT_scale=lhs_scales,
                 rhs=rhs[:, cols].bitcast(FP8X4),
                 rhs_scale=rhs_scales[:, cols],
                 start=True,
@@ -127,7 +131,7 @@ def tile_picked_densesendwind_none_po_kernel(
 
         def send(t, first, count):
             cols = slice(first, first + count)
-            y = product(w1, w1s, t, xq, xs, first, count)
+            y = product(w1[:, P * t : P * (t + 1)], w1s[:, P * t : P * (t + 1)], xq, xs, first, count)
             nc.scalar.activation(rl[:, t, cols], y, ACT.Relu)
             nc.vector.tensor_copy(sent[t][:].indirect(entries(n1_sb, first, count)), rl[:, t, cols])
             half = half_gs[:, t : t + 1] if t == LAST else -0.5
@@ -155,8 +159,8 @@ def tile_picked_densesendwind_none_po_kernel(
         nc.vector.tensor_copy(d_picked[:], d_table[:].indirect(k1_sb[:]))
         send(3, 0, S)
         combine_aside(2)
-        dq = keep.tile([P, H], U32, align_bytes=64)
-        deal(dq, d_picked, 0, PACK)
+        dq_first = keep.tile([P, P], U32, align_bytes=64)
+        deal(dq_first[:], d_picked, 0, 1)
 
         z_woven = [keep.tile([P, HALF, PACK], BF16, name=f"z_woven{i}", align_bytes=64) for i in range(2)]
         zq = keep.tile([P, S], U32, align_bytes=64)
@@ -165,25 +169,23 @@ def tile_picked_densesendwind_none_po_kernel(
         combine(LAST, HALF, HALF)
         combine(LAST, 0, HALF)
         nc.scalar.copy(z_woven[0][:, :, LAST], z_rows[:, LAST, 0:HALF])
-        nc.vector.tensor_copy(z_woven[1][:], z_rows[:, :, HALF:S].rearrange("p t j -> p j t"))
+        nc.vector.tensor_copy(
+            z_woven[1][:].rearrange("p (c i) t -> p c t i", i=PACK),
+            z_rows[:, :, HALF:S].rearrange("p t (c i) -> p c t i", i=PACK),
+        )
 
-        h = [keep.tile([P, S], F32, name=f"h{t}") for t in range(PACK)]
-        h_all = keep.tile([P, PACK, S], F32)
-        later = []
+        h = [keep.tile([P, 2 * S], F32, name=f"h{t}") for t in range(PACK)]
         for i in (1, 0):
             cols = slice(i * HALF, (i + 1) * HALF)
             nc.vector.quantize_mx(
                 out=zq[:, cols].bitcast(FP8X4), scales=zs[:, cols], in_=z_woven[i][:].rearrange("p j t -> p (j t)")
             )
-            acc = product(dq, d_plane, 0, zq, zs, i * HALF, HALF)
-            nc.scalar.activation(h[0][:, cols], acc, ACT.Copy, scale=0.0625)
-            later.append((h_all[:, 0, cols], acc))
+            nc.scalar.activation(h[0][:, cols], product(dq_first[:], d_plane[:, 0:P], zq, zs, i * HALF, HALF), ACT.Copy, scale=0.0625)
+        dq_rest = keep.tile([P, LAST * P], U32, name="z_woven0", align_bytes=64)
+        deal(dq_rest[:], d_picked, 1, PACK)
         for t in range(1, PACK):
-            acc = product(dq, d_plane, t, zq, zs, 0, S)
-            nc.scalar.activation(h[t][:], acc, ACT.Copy, scale=0.0625)
-            later.append((h_all[:, t, :], acc))
-        for dst, acc in later:
-            nc.scalar.activation(dst, acc, ACT.Copy, scale=0.0625)
+            acc = product(dq_rest[:, P * (t - 1) : P * t], d_plane[:, P * t : P * (t + 1)], zq, zs, 0, S)
+            nc.scalar.activation(h[t][:, 0:S], acc, ACT.Copy, scale=0.0625)
 
         out_rows = out_0.rearrange("(p t) j -> p t j", t=PACK)
         out_words = words_of(out_1)
@@ -192,15 +194,6 @@ def tile_picked_densesendwind_none_po_kernel(
 
         woven = [keep.tile([P, HALF, PACK], BF16, name=f"woven{i}", align_bytes=64) for i in range(2)]
 
-        def weave(engine_copy, res, first, count):
-            for i in range(2):
-                lo, hi = max(first, i * HALF), min(first + count, (i + 1) * HALF)
-                if lo < hi:
-                    engine_copy(
-                        woven[i][:, lo - i * HALF : hi - i * HALF, :],
-                        res[:, :, lo - first : hi - first].rearrange("p t j -> p j t"),
-                    )
-
         def hand_on(i):
             cols = slice(i * HALF, (i + 1) * HALF)
             nc.vector.quantize_mx(
@@ -208,27 +201,48 @@ def tile_picked_densesendwind_none_po_kernel(
             )
             nc.scalar.dma_start(out=out_words[:, cols], in_=oq[:, cols].bitcast(I32))
 
-        for first, count in OUT_CHUNKS:
+        at3 = keep.tile([P, PACK, S], F32)
+        diff = keep.tile([P, PACK, S], F32)
+        res = keep.tile([P, PACK, S], F32)
+
+        def fetch_n3(t, first, count):
+            nc.vector.tensor_copy(at3[:, t, first : first + count], h[t][:].indirect(entries(n3_sb, first, count)))
+
+        def fetch_n2(t, first, count):
             cols = slice(first, first + count)
-            at3 = keep.tile([P, PACK, count], F32, name=f"at3_{first}")
-            diff = keep.tile([P, PACK, count], F32, name=f"diff_{first}")
-            res = keep.tile([P, PACK, count], F32, name=f"res_{first}")
-            last = first + count == S
-            for t in range(PACK):
-                nc.vector.tensor_copy(at3[:, t, :], h[t][:].indirect(entries(n3_sb, first, count)))
-            for t in range(PACK):
-                nc.vector.tensor_tensor(
-                    diff[:, t, :], h[t][:].indirect(entries(n2_sb, first, count)), at3[:, t, :], ALU.subtract
-                )
-            if last:
-                for pair in (slice(0, 2), slice(2, 4)):
-                    nc.vector.tensor_tensor(res[:, pair, :], diff[:, pair, :], h_all[:, pair, cols], ALU.mult)
-                    nc.sync.dma_start(out=out_rows[:, pair, cols], in_=res[:, pair, :])
-                hand_on(0)
+            nc.vector.tensor_tensor(
+                diff[:, t, cols], h[t][:].indirect(entries(n2_sb, first, count)), at3[:, t, cols], ALU.subtract
+            )
+
+        def finish(engine, t, first, count):
+            cols = slice(first, first + count)
+            engine.tensor_tensor(res[:, t, cols], diff[:, t, cols], h[t][:, cols], ALU.mult)
+            nc.sync.dma_start(out=out_rows[:, t, cols], in_=res[:, t, cols])
+
+        def weave(copy, i, first, last):
+            cols = slice(i * HALF, (i + 1) * HALF)
+            copy(woven[i][:, :, first:last], res[:, first:last, cols].rearrange("p t j -> p j t"))
+
+        fetch_n3(0, 0, S)
+        for t in range(LAST):
+            fetch_n2(t, 0, S)
+            if t + 1 < LAST:
+                fetch_n3(t + 1, 0, S)
             else:
-                nc.gpsimd.tensor_tensor(res[:], diff[:], h_all[:, :, cols], ALU.mult)
-                nc.sync.dma_start(out=out_rows[:, :, cols], in_=res[:])
-            weave(nc.vector.tensor_copy if last else nc.scalar.copy, res, first, count)
+                fetch_n3(LAST, 0, HALF)
+                fetch_n3(LAST, HALF, HALF)
+            finish(nc.gpsimd, t, 0, S)
+            if t == 1:
+                weave(nc.scalar.copy, 0, 0, 2)
+                weave(nc.scalar.copy, 1, 0, 2)
+        weave(nc.scalar.copy, 0, 2, LAST)
+        fetch_n2(LAST, 0, HALF)
+        fetch_n2(LAST, HALF, HALF)
+        finish(nc.vector, LAST, 0, HALF)
+        finish(nc.vector, LAST, HALF, HALF)
+        weave(nc.scalar.copy, 0, LAST, PACK)
+        weave(nc.vector.tensor_copy, 1, 2, PACK)
+        hand_on(0)
         hand_on(1)
         for q in range(4):
             queue = nc.sync if q % 2 == 0 else nc.scalar

@@ -125,29 +125,35 @@ def tile_picked_densesendwind_none_po_kernel(
             return acc[:, 0:count]
 
         rl = keep.tile([P, PACK, S], F32)
-        yh = keep.tile([P, PACK, S], F32)
+        yh = keep.tile([P, LAST, S], F32)
+        yh_last = [keep.tile([P, HALF], F32, name=f"yh_last{i}", align_bytes=64) for i in range(2)]
         sent = [keep.tile([P, 2 * S], F32, name=f"sent{t}") for t in range(PACK)]
+        unscaled = keep.tile([P, LAST, S], F32)
         z_rows = keep.tile([P, PACK, S], BF16, align_bytes=64)
+        z_woven = [keep.tile([P, HALF, PACK], BF16, name=f"z_woven{i}", align_bytes=64) for i in range(2)]
 
         def send(t, first, count):
             cols = slice(first, first + count)
             y = product(w1[:, P * t : P * (t + 1)], w1s[:, P * t : P * (t + 1)], xq, xs, first, count)
             nc.scalar.activation(rl[:, t, cols], y, ACT.Relu)
             nc.vector.tensor_copy(sent[t][:].indirect(entries(n1_sb, first, count)), rl[:, t, cols])
-            half = half_gs[:, t : t + 1] if t == LAST else -0.5
-            nc.scalar.activation(yh[:, t, cols], y, ACT.Copy, scale=half)
-
-        def combine(t, first, count):
-            cols = slice(first, first + count)
-            nc.vector.scalar_tensor_tensor(
-                z_rows[:, t, cols], sent[t][:, cols], gs_sb[:, t : t + 1], yh[:, t, cols], ALU.mult, ALU.add
-            )
-
-        unscaled = keep.tile([P, LAST, S], F32)
+            if t < LAST:
+                nc.scalar.activation(yh[:, t, cols], y, ACT.Copy, scale=-0.5)
+            else:
+                for i in range(2):
+                    nc.scalar.activation(
+                        yh_last[i][:], y[:, i * HALF : (i + 1) * HALF], ACT.Copy, scale=half_gs[:, t : t + 1]
+                    )
 
         def combine_aside(t):
             nc.gpsimd.tensor_tensor(unscaled[:, t, :], sent[t][:, 0:S], yh[:, t, :], ALU.add)
             nc.scalar.activation(z_rows[:, t, :], unscaled[:, t, :], ACT.Copy, scale=gs_sb[:, t : t + 1])
+
+        def weave_z(i, first):
+            nc.scalar.copy(
+                z_woven[i][:, :, first : first + 2],
+                z_rows[:, first : first + 2, i * HALF : (i + 1) * HALF].rearrange("p t j -> p j t"),
+            )
 
         for c in (0, HALF):
             send(0, c, HALF)
@@ -155,33 +161,34 @@ def tile_picked_densesendwind_none_po_kernel(
         send(2, 0, S)
         combine_aside(0)
         combine_aside(1)
-        d_picked = keep.tile([P, H], U32, align_bytes=64)
-        nc.vector.tensor_copy(d_picked[:], d_table[:].indirect(k1_sb[:]))
-        send(3, 0, S)
+        send(LAST, 0, S)
+        weave_z(0, 0)
+        weave_z(1, 0)
         combine_aside(2)
+        for i in range(2):
+            cols = slice(i * HALF, (i + 1) * HALF)
+            nc.vector.scalar_tensor_tensor(
+                z_rows[:, LAST, cols], sent[LAST][:, cols], gs_sb[:, LAST:PACK], yh_last[i][:], ALU.mult, ALU.add
+            )
+            weave_z(i, 2)
+        d_picked = keep.tile([P, H], U32, name="yh_last0", align_bytes=64)
+        nc.vector.tensor_copy(d_picked[:], d_table[:].indirect(k1_sb[:]))
         dq_first = keep.tile([P, P], U32, align_bytes=64)
         deal(dq_first[:], d_picked, 0, 1)
 
-        z_woven = [keep.tile([P, HALF, PACK], BF16, name=f"z_woven{i}", align_bytes=64) for i in range(2)]
         zq = keep.tile([P, S], U32, align_bytes=64)
         zs = keep.tile([P, S], U8, align_bytes=64)
-        nc.scalar.copy(z_woven[0][:, :, 0:LAST], z_rows[:, 0:LAST, 0:HALF].rearrange("p t j -> p j t"))
-        combine(LAST, HALF, HALF)
-        combine(LAST, 0, HALF)
-        nc.scalar.copy(z_woven[0][:, :, LAST], z_rows[:, LAST, 0:HALF])
-        nc.vector.tensor_copy(
-            z_woven[1][:].rearrange("p (c i) t -> p c t i", i=PACK),
-            z_rows[:, :, HALF:S].rearrange("p t (c i) -> p c t i", i=PACK),
-        )
 
         h = [keep.tile([P, 2 * S], F32, name=f"h{t}") for t in range(PACK)]
-        for i in (1, 0):
-            cols = slice(i * HALF, (i + 1) * HALF)
+        for first, count in ((0, HALF), (HALF, HALF)):
+            cols = slice(first, first + count)
+            source = z_woven[first // HALF][:, first % HALF : first % HALF + count, :]
             nc.vector.quantize_mx(
-                out=zq[:, cols].bitcast(FP8X4), scales=zs[:, cols], in_=z_woven[i][:].rearrange("p j t -> p (j t)")
+                out=zq[:, cols].bitcast(FP8X4), scales=zs[:, cols], in_=source.rearrange("p j t -> p (j t)")
             )
-            nc.scalar.activation(h[0][:, cols], product(dq_first[:], d_plane[:, 0:P], zq, zs, i * HALF, HALF), ACT.Copy, scale=0.0625)
-        dq_rest = keep.tile([P, LAST * P], U32, name="z_woven0", align_bytes=64)
+            acc = product(dq_first[:], d_plane[:, 0:P], zq, zs, first, count)
+            nc.scalar.activation(h[0][:, cols], acc, ACT.Copy, scale=0.0625)
+        dq_rest = keep.tile([P, LAST * P], U32, name="z_woven1", align_bytes=64)
         deal(dq_rest[:], d_picked, 1, PACK)
         for t in range(1, PACK):
             acc = product(dq_rest[:, P * (t - 1) : P * t], d_plane[:, P * t : P * (t + 1)], zq, zs, 0, S)

@@ -52,21 +52,21 @@ def tile_picked_densesendwind_none_po_kernel(
         d_plane = keep.tile([P, H], U8, align_bytes=64)
         gs_sb = keep.tile([P, PACK], F32)
 
-        nc.vector.memset(dsc_table[:].bitcast(I32), 0)
+        nc.gpsimd.memset(dsc_table[:].bitcast(I32), 0)
+        nc.vector.memset(xs_table[:].bitcast(I32), 0)
+        nc.vector.memset(w1s_raw[:].bitcast(I32), 0)
         nc.vector.memset(d_plane[:].bitcast(I32), 0)
 
         def load_plane(dst, scales, q):
-            rows = scales[0, 4 * q : 4 * q + 4, :].bitcast(I32)
             nc.sync.dma_start(
-                out=dst[32 * q : 32 * q + 32, :].bitcast(I32),
-                in_=rows.unsqueeze(0).broadcast_to([8, 4, rows.shape[1]]),
+                out=dst[32 * q : 32 * q + 4, :].bitcast(I32), in_=scales[0, 4 * q : 4 * q + 4, :].bitcast(I32)
             )
 
         nc.sync.dma_start(k1_sb[:], k1)
+        nc.sync.dma_start(offs_sb[:], offs)
         nc.sync.dma_start(out=dsc_table[0:P:8, :].bitcast(I32), in_=d_scales[0].bitcast(I32))
         for q in range(4):
             load_plane(xs_table, x_scales, q)
-        nc.sync.dma_start(offs_sb[:], offs)
         nc.sync.dma_start(out=x_table[:].bitcast(I32), in_=words_of(x_words))
         nc.sync.dma_start(out=w1_raw[:].bitcast(I32), in_=words_of(w1_words))
         for q in range(4):

from contextlib import ExitStack

import concourse.mybir as mybir

K, T, S, H, G = 512, 2048, 512, 512, 2048
FLOPS = 2 * K * H * S + 2 * H * H * S

F32 = mybir.dt.float32
BF16 = mybir.dt.bfloat16
I32 = mybir.dt.int32
U32 = mybir.dt.uint32
U16 = mybir.dt.uint16
U8 = mybir.dt.uint8
FP8X4 = mybir.dt.float8_e4m3fn_x4
ALU = mybir.AluOpType
ACT = mybir.ActivationFunctionType

P = 128
PACK = 4
HALF = S // 2
LAST = PACK - 1
LIST = 16


def tile_picked_densesendwind_none_po_kernel(
    tc, x_words, x_scales, w1_words, w1_scales, gs, d_words, d_scales, offs, n1, k1, n2, n3, out_0, out_1, out_2
):
    nc = tc.nc

    def words_of(dram):
        return dram[0].rearrange("p c r -> p (c r)").bitcast(I32)

    def entries(lists, first, count):
        return lists[:, first // LIST : (first + count) // LIST]

    with ExitStack() as ctx:
        keep = ctx.enter_context(tc.tile_pool(name="keep", bufs=1))
        psum = ctx.enter_context(tc.psum_pool(name="psum", bufs=8))

        offs_sb = keep.tile([P, S // LIST], U16)
        n1_sb = keep.tile([P, S // LIST], U16)
        k1_sb = keep.tile([P, H // LIST], U16)
        n2_sb = keep.tile([P, S // LIST], U16)
        n3_sb = keep.tile([P, S // LIST], U16)

        x_table = keep.tile([P, T], U32, align_bytes=64)
        xs_table = keep.tile([P, T], U8, align_bytes=64)
        w1_raw = keep.tile([P, H], U32, align_bytes=64)
        w1s_raw = keep.tile([P, H], U8, align_bytes=64)
        d_table = keep.tile([P, G], U32, align_bytes=64)
        dsc_table = keep.tile([P, G], U8, align_bytes=64)
        d_plane = keep.tile([P, H], U8, align_bytes=64)
        gs_sb = keep.tile([P, PACK], F32)

        nc.gpsimd.memset(dsc_table[:].bitcast(I32), 0)
        nc.vector.memset(xs_table[:].bitcast(I32), 0)
        nc.vector.memset(w1s_raw[:].bitcast(I32), 0)
        nc.vector.memset(d_plane[:].bitcast(I32), 0)

        def load_plane(dst, scales, q):
            nc.sync.dma_start(
                out=dst[32 * q : 32 * q + 4, :].bitcast(I32), in_=scales[0, 4 * q : 4 * q + 4, :].bitcast(I32)
            )

        nc.sync.dma_start(k1_sb[:], k1)
        nc.sync.dma_start(offs_sb[:], offs)
        nc.sync.dma_start(out=dsc_table[0:P:8, :].bitcast(I32), in_=d_scales[0].bitcast(I32))
        for q in range(4):
            load_plane(xs_table, x_scales, q)
        nc.sync.dma_start(out=x_table[:].bitcast(I32), in_=words_of(x_words))
        nc.sync.dma_start(out=w1_raw[:].bitcast(I32), in_=words_of(w1_words))
        for q in range(4):
            load_plane(w1s_raw, w1_scales, q)
        nc.sync.dma_start(n1_sb[:], n1)
        nc.sync.dma_start(out=gs_sb[:], in_=gs.rearrange("(p t) o -> p (t o)", t=PACK))
        nc.sync.dma_start(out=d_table[:].bitcast(I32), in_=words_of(d_words))
        nc.sync.dma_start(n3_sb[:], n3)
        nc.sync.dma_start(n2_sb[:], n2)

        half_gs = keep.tile([P, PACK], F32)
        nc.scalar.activation(half_gs[:], gs_sb[:], ACT.Copy, scale=-0.5)

        def deal(dst, src, first, last):
            nc.vector.tensor_copy(
                out=dst.rearrange("p (t c i) -> p c t i", t=last - first, i=PACK),
                in_=src[:].rearrange("p (c i t) -> p c t i", t=PACK, i=PACK)[:, :, first:last, :],
            )

        def deal_bytes(dst, src, first, last):
            nc.vector.tensor_copy(
                out=dst.rearrange("p (t m) -> p t m", t=last - first),
                in_=src[:].rearrange("p (m t) -> p t m", t=PACK)[:, first:last, :],
            )

        ds_picked = keep.tile([P, H], U8, align_bytes=64)
        nc.vector.tensor_copy(ds_picked[:], dsc_table[:].indirect(k1_sb[:]))
        xs = keep.tile([P, S], U8, align_bytes=64)
        nc.vector.tensor_copy(xs[:], xs_table[:].indirect(offs_sb[:]))
        w1 = keep.tile([P, H], U32, align_bytes=64)
        w1s = keep.tile([P, H], U8, align_bytes=64)
        ds_dealt = keep.tile([P, H], U8, align_bytes=64)
        deal_bytes(ds_dealt[:], ds_picked, 0, PACK)
        xq = keep.tile([P, S], U32, align_bytes=64)
        nc.vector.tensor_copy(xq[:, 0:HALF], x_table[:].indirect(entries(offs_sb, 0, HALF)))
        deal(w1[:, 0 : 2 * P], w1_raw, 0, 2)
        deal_bytes(w1s[:, 0 : 2 * P], w1s_raw, 0, 2)
        nc.vector.tensor_copy(xq[:, HALF:S], x_table[:].indirect(entries(offs_sb, HALF, HALF)))
        deal(w1[:, 2 * P : H], w1_raw, 2, PACK)
        deal_bytes(w1s[:, 2 * P : H], w1s_raw, 2, PACK)
        for r in range(4):
            nc.sync.dma_start(out=d_plane[r:P:32, :].bitcast(I32), in_=ds_dealt[8 * r : P : 32, :].bitcast(I32))

        def product(lhs, lhs_scales, rhs, rhs_scales, first, count):
            acc = psum.tile([P, S], F32, name="acc")
            cols = slice(first, first + count)
            nc.tensor.matmul_mx(
                out=acc[:, 0:count],
                lhsT=lhs.bitcast(FP8X4),
                lhsT_scale=lhs_scales,
                rhs=rhs[:, cols].bitcast(FP8X4),
                rhs_scale=rhs_scales[:, cols],
                start=True,
                stop=True,
            )
            return acc[:, 0:count]

        rl = keep.tile([P, PACK, S], F32)
        yh = keep.tile([P, LAST, S], F32)
        yh_last = [keep.tile([P, HALF], F32, name=f"yh_last{i}", align_bytes=64) for i in range(2)]
        sent = [keep.tile([P, 2 * S], F32, name=f"sent{t}") for t in range(PACK)]
        unscaled = keep.tile([P, LAST, S], F32)
        z_rows = keep.tile([P, PACK, S], BF16, align_bytes=64)
        z_woven = [keep.tile([P, HALF, PACK], BF16, name=f"z_woven{i}", align_bytes=64) for i in range(2)]

        def send(t, first, count):
            cols = slice(first, first + count)
            y = product(w1[:, P * t : P * (t + 1)], w1s[:, P * t : P * (t + 1)], xq, xs, first, count)
            nc.scalar.activation(rl[:, t, cols], y, ACT.Relu)
            nc.vector.tensor_copy(sent[t][:].indirect(entries(n1_sb, first, count)), rl[:, t, cols])
            if t < LAST:
                nc.scalar.activation(yh[:, t, cols], y, ACT.Copy, scale=-0.5)
            else:
                for i in range(2):
                    nc.scalar.activation(
                        yh_last[i][:], y[:, i * HALF : (i + 1) * HALF], ACT.Copy, scale=half_gs[:, t : t + 1]
                    )

        def combine_aside(t):
            nc.gpsimd.tensor_tensor(unscaled[:, t, :], sent[t][:, 0:S], yh[:, t, :], ALU.add)
            nc.scalar.activation(z_rows[:, t, :], unscaled[:, t, :], ACT.Copy, scale=gs_sb[:, t : t + 1])

        def weave_z(i, first):
            nc.scalar.copy(
                z_woven[i][:, :, first : first + 2],
                z_rows[:, first : first + 2, i * HALF : (i + 1) * HALF].rearrange("p t j -> p j t"),
            )

        for c in (0, HALF):
            send(0, c, HALF)
            send(1, c, HALF)
        send(2, 0, S)
        combine_aside(0)
        combine_aside(1)
        send(LAST, 0, S)
        weave_z(0, 0)
        weave_z(1, 0)
        combine_aside(2)
        for i in range(2):
            cols = slice(i * HALF, (i + 1) * HALF)
            nc.vector.scalar_tensor_tensor(
                z_rows[:, LAST, cols], sent[LAST][:, cols], gs_sb[:, LAST:PACK], yh_last[i][:], ALU.mult, ALU.add
            )
            weave_z(i, 2)
        d_picked = keep.tile([P, H], U32, name="yh_last0", align_bytes=64)
        nc.vector.tensor_copy(d_picked[:], d_table[:].indirect(k1_sb[:]))
        dq_first = keep.tile([P, P], U32, align_bytes=64)
        deal(dq_first[:], d_picked, 0, 1)

        zq = keep.tile([P, S], U32, align_bytes=64)
        zs = keep.tile([P, S], U8, align_bytes=64)

        h = [keep.tile([P, 2 * S], F32, name=f"h{t}") for t in range(PACK)]
        for first, count in ((0, HALF), (HALF, HALF)):
            cols = slice(first, first + count)
            source = z_woven[first // HALF][:, first % HALF : first % HALF + count, :]
            nc.vector.quantize_mx(
                out=zq[:, cols].bitcast(FP8X4), scales=zs[:, cols], in_=source.rearrange("p j t -> p (j t)")
            )
            acc = product(dq_first[:], d_plane[:, 0:P], zq, zs, first, count)
            nc.scalar.activation(h[0][:, cols], acc, ACT.Copy, scale=0.0625)
        dq_rest = keep.tile([P, LAST * P], U32, name="z_woven1", align_bytes=64)
        deal(dq_rest[:], d_picked, 1, PACK)
        for t in range(1, PACK):
            acc = product(dq_rest[:, P * (t - 1) : P * t], d_plane[:, P * t : P * (t + 1)], zq, zs, 0, S)
            nc.scalar.activation(h[t][:, 0:S], acc, ACT.Copy, scale=0.0625)

        out_rows = out_0.rearrange("(p t) j -> p t j", t=PACK)
        out_words = words_of(out_1)
        oq = keep.tile([P, S], U32, align_bytes=64)
        os_plane = keep.tile([P, S], U8, align_bytes=64)

        woven = [keep.tile([P, HALF, PACK], BF16, name=f"woven{i}", align_bytes=64) for i in range(2)]

        def hand_on(i):
            cols = slice(i * HALF, (i + 1) * HALF)
            nc.vector.quantize_mx(
                out=oq[:, cols].bitcast(FP8X4), scales=os_plane[:, cols], in_=woven[i][:].rearrange("p j t -> p (j t)")
            )
            nc.scalar.dma_start(out=out_words[:, cols], in_=oq[:, cols].bitcast(I32))

        at3 = keep.tile([P, PACK, S], F32)
        diff = keep.tile([P, PACK, S], F32)
        res = keep.tile([P, PACK, S], F32)

        def fetch_n3(t, first, count):
            nc.vector.tensor_copy(at3[:, t, first : first + count], h[t][:].indirect(entries(n3_sb, first, count)))

        def fetch_n2(t, first, count):
            cols = slice(first, first + count)
            nc.vector.tensor_tensor(
                diff[:, t, cols], h[t][:].indirect(entries(n2_sb, first, count)), at3[:, t, cols], ALU.subtract
            )

        def finish(engine, t, first, count):
            cols = slice(first, first + count)
            engine.tensor_tensor(res[:, t, cols], diff[:, t, cols], h[t][:, cols], ALU.mult)
            nc.sync.dma_start(out=out_rows[:, t, cols], in_=res[:, t, cols])

        def weave(copy, i, first, last):
            cols = slice(i * HALF, (i + 1) * HALF)
            copy(woven[i][:, :, first:last], res[:, first:last, cols].rearrange("p t j -> p j t"))

        fetch_n3(0, 0, S)
        for t in range(LAST):
            fetch_n2(t, 0, S)
            if t + 1 < LAST:
                fetch_n3(t + 1, 0, S)
            else:
                fetch_n3(LAST, 0, HALF)
                fetch_n3(LAST, HALF, HALF)
            finish(nc.gpsimd, t, 0, S)
            if t == 1:
                weave(nc.scalar.copy, 0, 0, 2)
                weave(nc.scalar.copy, 1, 0, 2)
        weave(nc.scalar.copy, 0, 2, LAST)
        fetch_n2(LAST, 0, HALF)
        fetch_n2(LAST, HALF, HALF)
        finish(nc.vector, LAST, 0, HALF)
        finish(nc.vector, LAST, HALF, HALF)
        weave(nc.scalar.copy, 0, LAST, PACK)
        weave(nc.vector.tensor_copy, 1, 2, PACK)
        hand_on(0)
        hand_on(1)
        for q in range(4):
            queue = nc.sync if q % 2 == 0 else nc.scalar
            queue.dma_start(
                out=out_2[0, 4 * q : 4 * q + 4, :].bitcast(I32), in_=os_plane[32 * q : 32 * q + 4, :].bitcast(I32)
            )
